import numpy as np
import ml_dtypes


def mxq(x, axis, fmt="e4m3"):
    dtype, down = {"e4m3": (ml_dtypes.float8_e4m3fn, 7), "e5m2": (ml_dtypes.float8_e5m2, 14)}[fmt]
    v = np.moveaxis(np.asarray(x, np.float32).astype(ml_dtypes.bfloat16).astype(np.float64), axis, -1)
    blocks = v.reshape(v.shape[:-1] + (-1, 32))
    amax = np.abs(blocks).max(-1, keepdims=True)
    byte = np.maximum(np.where(amax > 0, np.frexp(amax)[1] - 1 + 127, 0) - down, 1)
    scale = np.exp2(byte - 127.0)
    codes = (blocks / scale).astype(np.float32).astype(dtype).astype(np.float64)
    return np.moveaxis((codes * scale).reshape(v.shape), -1, axis)


WIDE = False


def mx_kscale(k):
    if not WIDE:
        return np.ones(k)
    levels = np.array([10, -10, 5, -5, 0])
    if k % 512:
        return np.exp2(np.random.permutation(np.resize(levels, k // 32))).repeat(32)
    a = np.empty((k // 512, 16))
    for p in range(k // 512):
        a[p, :8] = np.random.permutation(np.resize(levels, 8))
        for g in range(8):
            far = levels[np.abs(levels - a[p, g]) >= 10]
            a[p, g + 8] = far[np.random.randint(len(far))]
    return np.exp2(a.ravel()).repeat(32)


def f64(x):
    return np.asarray(x).astype(np.float64)


def striped(idx):
    return np.tile(idx.reshape(-1, 16).T, (8, 1)).astype(np.uint16)


def unstriped(offs):
    return offs[:16].T.reshape(-1).astype(np.int64)


E2M1 = np.array([0.0, 0.5, 1.0, 1.5, 2.0, 3.0, 4.0, 6.0, -0.0, -0.5, -1.0, -1.5, -2.0, -3.0, -4.0, -6.0])


def pack_weight(w, fmt):
    k, n = w.shape
    w = f64(np.asarray(w, np.float32).astype(ml_dtypes.bfloat16)).reshape(k // 32, 32, n)
    amax = np.abs(w).max(1)
    if fmt == "e4m3":
        byte = np.frexp(amax)[1] - 1 + 127 - 7
    else:
        mant, ex = np.frexp(amax / 6.0)
        byte = np.where(mant > 0.5, ex, ex - 1) + 127
    byte = np.clip(np.where(amax > 0, byte, 1), 1, 254)
    scaled = (w * np.exp2(127.0 - byte)[:, None, :]).reshape(k, n).astype(np.float32)
    by_word = np.ascontiguousarray(scaled.reshape(k // 512, 128, 4, n).transpose(0, 1, 3, 2))
    if fmt == "e4m3":
        words = by_word.astype(ml_dtypes.float8_e4m3fn).view(np.uint8)
    else:
        c = by_word.astype(ml_dtypes.float4_e2m1fn).view(np.uint8) & 0xF
        words = (c[..., 0::2] | (c[..., 1::2] << 4)).reshape(k // 512, 128, 2 * n)
    return np.ascontiguousarray(words), np.ascontiguousarray(byte.astype(np.uint8).reshape(k // 512, 16, n))


def unpack_weight(words, scales, fmt):
    g, _, n = scales.shape
    words = np.ascontiguousarray(words).reshape(g, 128, n, -1)
    if fmt == "e4m3":
        vals = words.view(ml_dtypes.float8_e4m3fn).astype(np.float64)
    else:
        nib = np.empty((g, 128, n, 4), np.uint8)
        nib[..., 0::2] = words & 0xF
        nib[..., 1::2] = words >> 4
        vals = E2M1[nib]
    vals = vals * np.repeat(np.exp2(scales.astype(np.float64) - 127.0), 8, axis=1)[..., None]
    return vals.transpose(0, 1, 3, 2).reshape(g * 512, n)


def gelu(v):
    return 0.5 * v * (1.0 + np.tanh(np.sqrt(2.0 / np.pi) * (v + 0.044715 * v**3)))


K, KA, H, T, S, T2, P = 1024, 512, 1024, 2048, 1024, 2048, 512

def setup_inputs():
    n = np.random.standard_normal
    s, u = mx_kscale(K)[:, None], mx_kscale(H)[:, None]
    tab_words, tab_scales = pack_weight(n((K, T)) * s, "e4m3")
    w4_words, w4_scales = pack_weight(n((KA, H)) / np.sqrt(K) / s[:KA] * u.T, "e2m1")
    w1 = n((K - KA, H)) / np.sqrt(K) / s[KA:] * u.T
    return {"tab_words": tab_words, "tab_scales": tab_scales,
            "w4_words": w4_words, "w4_scales": w4_scales,
            "w1": w1.astype(np.float32),
            "supplier": (n((H, S)) * u).astype(np.float32),
            "page0": (n((H, T2)) * u).astype(np.float32),
            "wgs": np.exp(0.3 * n((128, S))).astype(np.float32),
            "gain": (n(H) / np.sqrt(H) / u[:, 0] ** 2).astype(np.float32),
            "pig": (0.8 * n(P)).astype(np.float32),
            "disp": (1.5 * np.exp(0.4 * n(P))).astype(np.float32),
            "offs": striped(np.random.permutation(T)[:S]),
            "offs2": striped(np.random.permutation(T2)[:S]),
            "offs3": striped(np.random.permutation(T2)[:P]),
            "offs4": striped(np.random.permutation(T2)[:P])}

def reference(tab_words, tab_scales, w4_words, w4_scales, w1, supplier, page0, wgs, gain, pig, disp,
              offs, offs2, offs3, offs4):
    v = unpack_weight(tab_words, tab_scales, "e4m3")[:, unstriped(offs)]
    w4 = unpack_weight(w4_words, w4_scales, "e2m1")
    f = w4.T @ v[:KA] + mxq(f64(w1), 0, "e4m3").T @ v[KA:]
    h = np.maximum(f, f64(supplier))
    page = f64(page0).copy()
    page[:, unstriped(offs2)] = np.tile(f64(wgs), (H // 128, 1)) * h
    x1 = page[:, unstriped(offs3)]
    x2 = np.abs(page[:, unstriped(offs4)]) * f64(gain)[:, None]
    e = mxq(x1, 0, "e4m3").T @ mxq(x2, 0, "e4m3")
    z = (e + f64(pig)[:, None]) * f64(disp)[None, :]
    return 1.0 / (1.0 + np.exp(-z))

from contextlib import ExitStack

import concourse.mybir as mybir

K, KA, H, T, S, T2, R = 1024, 512, 1024, 2048, 1024, 2048, 512
FLOPS = 2 * K * H * S + 2 * H * R * R

F32 = mybir.dt.float32
BF16 = mybir.dt.bfloat16
I32 = mybir.dt.int32
U32 = mybir.dt.uint32
U16 = mybir.dt.uint16
U8 = mybir.dt.uint8
FP8X4 = mybir.dt.float8_e4m3fn_x4
FP4X4 = mybir.dt.float4_e2m1fn_x4
ALU = mybir.AluOpType
ACT = mybir.ActivationFunctionType

P = 128
PACK = 4
PASS = P * PACK
BANK = 512
TILES = H // P


def tile_list_pigment_dispersant_ratings_kernel(
    tc, tab_words, tab_scales, w4_words, w4_scales, w1, supplier, page0, wgs, gain, pig, disp,
    offs, offs2, offs3, offs4, out,
):
    nc = tc.nc
    with ExitStack() as ctx:
        keep = ctx.enter_context(tc.tile_pool(name="keep", bufs=1))
        pair = ctx.enter_context(tc.tile_pool(name="pair", bufs=2))
        stream = ctx.enter_context(tc.tile_pool(name="stream", bufs=6))
        outs = ctx.enter_context(tc.tile_pool(name="outs", bufs=4))
        psum_f = ctx.enter_context(tc.psum_pool(name="psum_f", bufs=4))
        psum_e = ctx.enter_context(tc.psum_pool(name="psum_e", bufs=1))

        list1 = keep.tile([P, S // 16], U16, name="list1")
        list2 = keep.tile([P, S // 16], U16, name="list2")
        list3 = keep.tile([P, R // 16], U16, name="list3")
        list4 = keep.tile([P, R // 16], U16, name="list4")

        w4_raw = keep.tile([P, 2 * H], U8, name="w4_raw", align_bytes=64)
        w4_sraw = keep.tile([P, H], U8, name="w4_sraw", align_bytes=64)
        tab_s = keep.tile([P, T], U8, name="tab_s", align_bytes=64)
        tab_w = [keep.tile([P, T], U32, name=f"tab_w{a}", align_bytes=64) for a in range(2)]
        nc.vector.memset(tab_s[:].bitcast(I32), 0)
        nc.gpsimd.memset(w4_sraw[:].bitcast(I32), 0)

        nc.sync.dma_start(list1[:], offs)
        nc.sync.dma_start(w4_raw[:].bitcast(I32), w4_words[0].bitcast(I32))
        for a in range(2):
            nc.sync.dma_start(tab_w[a][:].bitcast(I32), tab_words[a].rearrange("p t i -> p (t i)").bitcast(I32))
        for q in range(4):
            nc.gpsimd.dma_start(tab_s[32 * q : 32 * q + 8, :].bitcast(I32),
                                tab_scales[:, 4 * q : 4 * q + 4, :].bitcast(I32))
        for q in range(4):
            nc.scalar.dma_start(w4_sraw[32 * q : 32 * q + 4, :].bitcast(I32),
                                w4_scales[0, 4 * q : 4 * q + 4, :].bitcast(I32))

        w1_rows = w1.rearrange("(p i) c -> p i c", i=PACK)
        sup_rows = supplier.rearrange("(b p t) j -> b t p j", p=P, t=PACK)
        page_rows = page0.rearrange("(b p t) c -> b t p c", p=P, t=PACK)
        wgs_rows = wgs.rearrange("(q t) j -> q t j", t=PACK)

        w1_raw = {}
        sup = {}
        page = {}

        def load_w1(b):
            w1_raw[b] = pair.tile([P, PACK, PASS], F32, name="w1_raw")
            nc.sync.dma_start(w1_raw[b][:], w1_rows[:, :, b * PASS : (b + 1) * PASS])

        def load_sup(i):
            sup[i] = stream.tile([P, S], F32, name="sup")
            nc.sync.dma_start(sup[i][:], sup_rows[i // PACK, i % PACK])

        def load_page(i):
            page[i] = stream.tile([P, T2], F32, name="page")
            nc.sync.dma_start(page[i][:], page_rows[i // PACK, i % PACK])

        wgs_first = keep.tile([P, S], F32, name="wgs_first")
        wgs_rest = keep.tile([P, PACK - 1, S], F32, name="wgs_rest")
        gain_sb = keep.tile([P, 2, PACK], F32, name="gain_sb")
        pig_sb = keep.tile([P, R // P], F32, name="pig_sb")
        disp_sb = keep.tile([P, R], F32, name="disp_sb")

        load_w1(0)
        load_sup(0)
        for g in (0, 2, 1, 3):
            nc.sync.dma_start(wgs_first[32 * g : 32 * g + 32, :], wgs_rows[:, 0, :])
        nc.sync.dma_start(list2[:], offs2)
        load_page(0)
        load_sup(1)
        nc.sync.dma_start(list4[:], offs4)
        nc.sync.dma_start(list3[:], offs3)
        nc.sync.dma_start(gain_sb[:], gain.rearrange("(b p t) -> p b t", p=P, t=PACK))
        for g in (0, 2, 1, 3):
            nc.sync.dma_start(wgs_rest[32 * g : 32 * g + 32, :, :], wgs_rows[:, 1:PACK, :])
        load_page(1)
        load_sup(2)
        load_page(2)
        load_sup(3)
        load_w1(1)

        w4_codes = keep.tile([P, 2 * H], U8, name="w4_codes", align_bytes=64)
        w4_s = keep.tile([P, H], U8, name="w4_s", align_bytes=64)
        v_codes = [keep.tile([P, S], U32, name=f"v_codes{a}", align_bytes=64) for a in range(2)]
        v_s = [keep.tile([P, BANK], U8, name=f"v_s{u}", align_bytes=64) for u in range(2)]
        w1_codes = [keep.tile([P, PASS], U32, name=f"w1_codes{b}", align_bytes=64) for b in range(2)]
        w1_s = [keep.tile([P, PASS], U8, name=f"w1_s{b}", align_bytes=64) for b in range(2)]

        w1_woven = {}

        def weave_w1(b):
            w1_woven[b] = keep.tile([P, PACK, P, PACK], BF16, name="w1_woven", align_bytes=64)
            nc.scalar.copy(w1_woven[b][:].rearrange("p t m i -> p m t i"),
                           w1_raw[b][:].rearrange("p i (m t) -> p m t i", t=PACK))

        def quantize_w1(b):
            nc.vector.quantize_mx(out=w1_codes[b][:].bitcast(FP8X4), scales=w1_s[b][:],
                                  in_=w1_woven[b][:].rearrange("p t m i -> p (t m i)"))

        nc.vector.tensor_copy(w4_codes[:].rearrange("p (b t q e) -> p b t q e", b=2, t=PACK, e=2),
                              w4_raw[:].rearrange("p (b q t e) -> p b t q e", b=2, t=PACK, e=2))
        weave_w1(0)
        for a in range(2):
            nc.vector.tensor_copy(v_codes[a][:], tab_w[a][:].indirect(list1[:]))
        nc.vector.tensor_copy(v_s[0][:], tab_s[:].indirect(list1[:, 0:32]))
        nc.vector.tensor_copy(w4_s[:].rearrange("p (b t q) -> p b t q", b=2, t=PACK),
                              w4_sraw[:].rearrange("p (b q t) -> p b t q", b=2, t=PACK))
        quantize_w1(0)
        nc.vector.tensor_copy(v_s[1][:], tab_s[:].indirect(list1[:, 32:64]))

        h = {}

        def features(i):
            b, t = divmod(i, PACK)
            h[i] = pair.tile([P, S], F32, name="h")
            for u in range(2):
                cols = slice(u * BANK, (u + 1) * BANK)
                f = psum_f.tile([P, BANK], F32, name="f")
                nc.tensor.matmul_mx(out=f[:], lhsT=w4_codes[:, 2 * P * i : 2 * P * (i + 1)].bitcast(FP4X4),
                                    lhsT_scale=w4_s[:, P * i : P * (i + 1)],
                                    rhs=v_codes[0][:, cols].bitcast(FP8X4), rhs_scale=v_s[u][:],
                                    start=True, stop=False)
                nc.tensor.matmul_mx(out=f[:], lhsT=w1_codes[b][:, P * t : P * (t + 1)].bitcast(FP8X4),
                                    lhsT_scale=w1_s[b][:, P * t : P * (t + 1)],
                                    rhs=v_codes[1][:, cols].bitcast(FP8X4), rhs_scale=v_s[u][4:P, :],
                                    start=False, stop=True)
                nc.vector.tensor_tensor(h[i][:, cols], f[:], sup[i][:, cols], ALU.max)

        e = [psum_e.tile([P, R], F32, name=f"e{m}") for m in range(R // P)]

        features(0)
        for b in range(2):
            x1_planes = pair.tile([P, PACK, R], BF16, name="x1_planes")
            x1_woven = pair.tile([P, R, PACK], BF16, name="x1_woven", align_bytes=64)
            x2_woven = pair.tile([P, R, PACK], BF16, name="x2_woven", align_bytes=64)
            for t in range(PACK):
                i = b * PACK + t
                factor = wgs_first[:] if t == 0 else wgs_rest[:, t - 1, :]
                nc.vector.tensor_tensor(page[i][:].indirect(list2[:]), h[i][:], factor, ALU.mult)
                if i + 3 < TILES:
                    load_page(i + 3)
                if i + 4 < TILES:
                    load_sup(i + 4)
                if i == 1:
                    weave_w1(1)
                if i == 2:
                    quantize_w1(1)
                if i == 4:
                    with nc.allow_non_contiguous_dma(reason="one value a partition"):
                        nc.sync.dma_start(pig_sb[:], pig.rearrange("(m p) -> p m", p=P))
                    nc.sync.dma_start(disp_sb[:], disp.partition_broadcast(P))
                if i + 1 < TILES:
                    features(i + 1)
                picked = pair.tile([P, R], F32, name="picked")
                nc.vector.tensor_copy(picked[:], page[i][:].indirect(list4[:]))
                nc.vector.tensor_copy(x1_planes[:, t, :], page[i][:].indirect(list3[:]))
                size = pair.tile([P, R], F32, name="size")
                nc.scalar.activation(size[:], picked[:], ACT.Abs)
                nc.scalar.activation(x2_woven[:, :, t], size[:], ACT.Copy, scale=gain_sb[:, b, t : t + 1])

            woven_view = x1_woven[:].rearrange("p (c i) t -> p c t i", i=4)
            planes_view = x1_planes[:].rearrange("p t (c i) -> p c t i", i=4)
            if b == 0:
                nc.scalar.copy(woven_view, planes_view)
            else:
                nc.vector.tensor_copy(woven_view, planes_view)
            x1_codes = pair.tile([P, R], U32, name="x1_codes", align_bytes=64)
            x1_s = pair.tile([P, R], U8, name="x1_s", align_bytes=64)
            x2_codes = pair.tile([P, R], U32, name="x2_codes", align_bytes=64)
            x2_s = pair.tile([P, R], U8, name="x2_s", align_bytes=64)
            nc.vector.quantize_mx(out=x2_codes[:].bitcast(FP8X4), scales=x2_s[:],
                                  in_=x2_woven[:].rearrange("p c t -> p (c t)"))
            nc.vector.quantize_mx(out=x1_codes[:].bitcast(FP8X4), scales=x1_s[:],
                                  in_=x1_woven[:].rearrange("p c t -> p (c t)"))
            for m in range(R // P):
                rows = slice(m * P, (m + 1) * P)
                nc.tensor.matmul_mx(out=e[m][:], lhsT=x1_codes[:, rows].bitcast(FP8X4), lhsT_scale=x1_s[:, rows],
                                    rhs=x2_codes[:].bitcast(FP8X4), rhs_scale=x2_s[:],
                                    start=(b == 0), stop=(b == 1))

        for m in range(R // P):
            z = outs.tile([P, R], F32, name="z")
            nc.vector.scalar_tensor_tensor(z[:], e[m][:], pig_sb[:, m : m + 1], disp_sb[:], ALU.add, ALU.mult)
            rating = outs.tile([P, R], F32, name="rating")
            nc.scalar.activation(rating[:], z[:], ACT.Sigmoid)
            nc.sync.dma_start(out[m * P : (m + 1) * P, :], rating[:])
